import numpy as np, ml_dtypes
CORES = [1,3,5,9,11,13]
N = 6
DEG, TK = 5, 128
MASK = [[0,2,3,4,5],[0,1,3,4,5],[1,2,3,4,5],[0,1,3,4,5],[0,1,3,4,5],[0,2,3,4,5]]
def setup_inputs(rng):
    return {"x": rng.standard_normal((N, 128, TK), dtype=np.float32).astype(ml_dtypes.bfloat16), "w": rng.standard_normal((N, 128, DEG * 128), dtype=np.float32).astype(ml_dtypes.bfloat16)}
def setup_inputs_big(rng):
    d = setup_inputs(rng)
    for k in ("x", "w"): d[k] = (d[k].astype(np.float32) * 1024.0).astype(d[k].dtype)
    return d
def setup_inputs_small(rng):
    d = setup_inputs(rng)
    for k in ("x", "w"): d[k] = (d[k].astype(np.float32) * (1 / 1024.0)).astype(d[k].dtype)
    return d
def setup_inputs_apart(rng):
    d = setup_inputs(rng)
    f = (10.0 ** rng.permutation(np.linspace(-1.5, 1.5, N))).astype(np.float32).reshape(N, 1, 1)
    for k in ("x", "w"): d[k] = (d[k].astype(np.float32) * f).astype(d[k].dtype)
    return d
def reference(x, w):
    X, W = x.astype(np.float64), w.astype(np.float64)
    y = np.zeros((N, 128, TK))
    for r in range(N):
        for i, j in enumerate(MASK[r]):
            y[r] += W[r][:, 128 * i:128 * i + 128].T @ X[j]
    return {"y": y.astype(ml_dtypes.bfloat16 if x.dtype != np.float64 else np.float64)}

@@ -1,0 +1,148 @@
+from concourse.bass import DstId, RemoteDMATransfer
+
+TK = 128
+DEG = 5
+
+N_HELP = 16
+N_NEAR = 16
+N_FAR = 8
+
+SCRATCH = {
+    "xg": ("sbuf", [128, DEG * TK], "bfloat16"),
+    "wb": ("sbuf", [128, DEG * TK], "bfloat16"),
+    "acc": ("psum", [128, TK], "float32"),
+    "yo": ("sbuf", [128, TK], "bfloat16"),
+}
+SEMAPHORES = ["ldx", "ldw", "near", "far", "sent", "mm", "cp", "st"]
+
+
+def _pick(full, n, skip=0):
+    bits = [b for b in range(full.bit_length()) if (full >> b) & 1][skip:skip + n]
+    assert len(bits) == n
+    m = 0
+    for b in bits:
+        m |= 1 << b
+    return m
+
+
+def _plan(T, topo):
+    cores = list(T.cores)
+    need = T.tables["MASK"]
+    n = len(cores)
+    chip = [topo.chip(c) for c in cores]
+    lay = []
+    for r in range(n):
+        far = sorted((j for j in need[r] if chip[j] != chip[r]), key=lambda j: (chip[j], j))
+        lay.append(far + sorted(j for j in need[r] if chip[j] == chip[r]))
+        assert r in need[r]
+    jobs = {}
+    helper_in = {}
+    everyone = range(topo.CHIPS * topo.CORES_PER_CHIP)
+    for r in range(n):
+        for s in sorted(set(chip[j] for j in lay[r] if chip[j] != chip[r])):
+            members = [j for j in lay[r] if chip[j] == s]
+            cands = []
+            for c in everyone:
+                if topo.chip(c) != s or c in jobs or not topo.may_write(c, cores[r]):
+                    continue
+                q = T.rank_of(c)
+                at = 0
+                if q is not None:
+                    if members[0] not in lay[q]:
+                        continue
+                    at = lay[q].index(members[0])
+                    if lay[q][at:at + len(members)] != members:
+                        continue
+                cands.append((topo.die(c) != topo.die(cores[r]), q is None, c, at))
+            _, is_helper, c, at = min(cands)
+            jobs[c] = (cores[r], at, lay[r].index(members[0]), len(members))
+            if is_helper:
+                helper_in[c] = members
+    to_help, to_near = {}, {}
+    for j in range(n):
+        me = cores[j]
+        h = [(c, m.index(j)) for c, m in helper_in.items() if j in m]
+        h.sort(key=lambda e: (topo.die(e[0]) != topo.die(me), e[0]))
+        k = [(cores[r], lay[r].index(j)) for r in range(n) if r != j and chip[r] == chip[j] and j in need[r]]
+        k.sort(key=lambda e: (e[0] not in jobs, e[0]))
+        to_help[me], to_near[me] = h, k
+    near = {}
+    for me in cores:
+        for c, _ in to_help[me]:
+            near[c] = near.get(c, 0) + N_HELP
+        for c, _ in to_near[me]:
+            near[c] = near.get(c, 0) + N_NEAR
+    return lay, jobs, to_help, to_near, near
+
+
+def _cols(first, tiles=1):
+    return slice(first * TK, (first + tiles) * TK)
+
+
+def rank_program(g, core, T, topo):
+    lay, jobs, to_help, to_near, near = _plan(T, topo)
+    rank = T.rank_of(core)
+    S = T.sem
+    sent = 0
+
+    if rank is not None:
+        own = lay[rank].index(rank)
+        g.sync.dma_start(T.xg[:, _cols(own)], T.x[:, :]).then_inc(S.ldx, 16)
+        g.sync.dma_start(T.wb[:, :], T.w[:, :]).then_inc(S.ldw, 16)
+
+        g.wait_ge(S.ldx, 16)
+        for dests, eng in ((to_help[core], N_HELP), (to_near[core], N_NEAR)):
+            if not dests:
+                continue
+            full = topo.mask(core, dests[0][0])
+            for c, _ in dests:
+                full &= topo.mask(core, c)
+            g.remote_dma_fused(
+                [RemoteDMATransfer(
+                    dst_ids=[DstId(rid=topo.addr(c)[0], pnc=topo.addr(c)[1]) for c, _ in dests],
+                    dma_engine_mask=_pick(full, eng),
+                    remote_sem=S.near,
+                    srcs=[T.xg[:, _cols(own)]],
+                    dsts=[T.xg[:, _cols(slot)] for _, slot in dests],
+                    alu_op=0)],
+                local_sem=S.sent)
+            sent += eng
+
+    if core in jobs:
+        dst, at, slot, tiles = jobs[core]
+        g.wait_ge(S.near, near[core])
+        rid, pid, _ = topo.addr(dst)
+        g.remote_dma(out_ap=T.xg[:, _cols(slot, tiles)], in_ap=T.xg[:, _cols(at, tiles)],
+                     remote_sem=S.far, local_sem=S.sent, pid=pid, routing_id=rid,
+                     dma_engine_mask=_pick(topo.mask(core, dst), N_FAR))
+        sent += N_FAR
+
+    if sent:
+        g.wait_ge(S.sent, sent)
+
+    if rank is None:
+        return
+
+    need = T.tables["MASK"][rank]
+    mine = topo.chip(core)
+    here = [j for j in lay[rank] if j != rank and topo.chip(T.cores[j]) == mine]
+    there = [j for j in lay[rank] if topo.chip(T.cores[j]) != mine]
+    te = g.tensor
+    te.wait_ge(S.ldw, 16)
+    te.wait_ge(S.ldx, 16)
+    seq = [(rank, None)] + [(j, "near") for j in here] + [(j, "far") for j in there]
+    waited = set()
+    for k, (j, sem) in enumerate(seq):
+        if sem is not None and sem not in waited:
+            waited.add(sem)
+            te.wait_ge(S[sem], near[core] if sem == "near" else N_FAR)
+        mm = te.matmul(T.acc[:, :], T.wb[:, _cols(need.index(j))], T.xg[:, _cols(lay[rank].index(j))],
+                       k == 0, k == len(seq) - 1)
+    mm.then_inc(S.mm, 1)
+
+    g.vector.wait_ge(S.mm, 1)
+    g.vector.tensor_copy(T.yo[:, :], T.acc[:, :]).then_inc(S.cp, 1)
+
+    g.scalar.wait_ge(S.cp, 1)
+    g.scalar.dma_start(T.y[:, :], T.yo[:, :]).then_inc(S.st, 16)
+    g.scalar.wait_ge(S.st, 16)

@@ -3,8 +3,9 @@ from concourse.bass import DstId, RemoteDMATransfer
 TK = 128
 DEG = 5
 
-N_HELP = 16
-N_NEAR = 16
+N_HELP = 8
+N_DIR = 8
+N_NEAR = 8
 N_FAR = 8
 
 SCRATCH = {
@@ -13,11 +14,11 @@ SCRATCH = {
     "acc": ("psum", [128, TK], "float32"),
     "yo": ("sbuf", [128, TK], "bfloat16"),
 }
-SEMAPHORES = ["ldx", "ldw", "near", "far", "sent", "mm", "cp", "st"]
+SEMAPHORES = ["ldx", "ldw", "near", "dir", "far", "sent", "mm", "cp", "st"]
 
 
-def _pick(full, n, skip=0):
-    bits = [b for b in range(full.bit_length()) if (full >> b) & 1][skip:skip + n]
+def _pick(full, n):
+    bits = [b for b in range(full.bit_length()) if (full >> b) & 1][:n]
     assert len(bits) == n
     m = 0
     for b in bits:
@@ -30,57 +31,87 @@ def _plan(T, topo):
     need = T.tables["MASK"]
     n = len(cores)
     chip = [topo.chip(c) for c in cores]
+    def way(j, r):
+        if chip[j] == chip[r]:
+            return "near"
+        return "dir" if topo.may_write(cores[j], cores[r]) else "far"
     lay = []
     for r in range(n):
-        far = sorted((j for j in need[r] if chip[j] != chip[r]), key=lambda j: (chip[j], j))
-        lay.append(far + sorted(j for j in need[r] if chip[j] == chip[r]))
         assert r in need[r]
+        lay.append(sorted((j for j in need[r] if way(j, r) == "far"), key=lambda j: (chip[j], j))
+                   + sorted(j for j in need[r] if way(j, r) == "dir") + [r]
+                   + sorted(j for j in need[r] if way(j, r) == "near" and j != r))
     jobs = {}
     helper_in = {}
     everyone = range(topo.CHIPS * topo.CORES_PER_CHIP)
     for r in range(n):
-        for s in sorted(set(chip[j] for j in lay[r] if chip[j] != chip[r])):
-            members = [j for j in lay[r] if chip[j] == s]
+        for s in sorted(set(chip[j] for j in lay[r] if way(j, r) == "far")):
+            members = [j for j in lay[r] if way(j, r) == "far" and chip[j] == s]
             cands = []
             for c in everyone:
-                if topo.chip(c) != s or c in jobs or not topo.may_write(c, cores[r]):
+                if topo.chip(c) != s or not topo.may_write(c, cores[r]):
                     continue
                 q = T.rank_of(c)
-                at = 0
-                if q is not None:
-                    if members[0] not in lay[q]:
-                        continue
-                    at = lay[q].index(members[0])
-                    if lay[q][at:at + len(members)] != members:
-                        continue
-                cands.append((topo.die(c) != topo.die(cores[r]), q is None, c, at))
-            _, is_helper, c, at = min(cands)
-            jobs[c] = (cores[r], at, lay[r].index(members[0]), len(members))
+                if q is None and c in jobs:
+                    continue
+                if q is not None and not all(j in lay[q] for j in members):
+                    continue
+                cands.append((topo.die(c) != topo.die(cores[r]), q is None, c))
+            _, is_helper, c = min(cands)
+            at = 0
             if is_helper:
                 helper_in[c] = members
-    to_help, to_near = {}, {}
+            else:
+                q = T.rank_of(c)
+                at = lay[q].index(members[0])
+                assert lay[q][at:at + len(members)] == members
+            jobs.setdefault(c, {}).setdefault((at, len(members)), []).append((cores[r], lay[r].index(members[0])))
+    calls = {}
     for j in range(n):
         me = cores[j]
         h = [(c, m.index(j)) for c, m in helper_in.items() if j in m]
         h.sort(key=lambda e: (topo.die(e[0]) != topo.die(me), e[0]))
-        k = [(cores[r], lay[r].index(j)) for r in range(n) if r != j and chip[r] == chip[j] and j in need[r]]
+        d = [(cores[r], lay[r].index(j)) for r in range(n) if j in need[r] and way(j, r) == "dir"]
+        k = [(cores[r], lay[r].index(j)) for r in range(n) if j in need[r] and r != j and way(j, r) == "near"]
         k.sort(key=lambda e: (e[0] not in jobs, e[0]))
-        to_help[me], to_near[me] = h, k
-    near = {}
+        off = 0
+        for c, _ in d:
+            off |= topo.mask(me, c)
+        calls[me] = [c for c in ((h, N_HELP, "near", off), (d, N_DIR, "dir", 0), (k, N_NEAR, "near", off)) if c[0]]
+    count = {}
     for me in cores:
-        for c, _ in to_help[me]:
-            near[c] = near.get(c, 0) + N_HELP
-        for c, _ in to_near[me]:
-            near[c] = near.get(c, 0) + N_NEAR
-    return lay, jobs, to_help, to_near, near
+        for dests, eng, sem, _ in calls[me]:
+            for c, _ in dests:
+                count[c, sem] = count.get((c, sem), 0) + eng
+    for c in jobs:
+        for dests in jobs[c].values():
+            for d, _ in dests:
+                count[d, "far"] = count.get((d, "far"), 0) + N_FAR
+    return lay, way, jobs, calls, count
 
 
 def _cols(first, tiles=1):
     return slice(first * TK, (first + tiles) * TK)
 
 
+def _send(g, core, topo, T, src, dests, tiles, eng, sem, avoid=0):
+    full = topo.mask(core, dests[0][0])
+    for c, _ in dests:
+        full &= topo.mask(core, c)
+    g.remote_dma_fused(
+        [RemoteDMATransfer(
+            dst_ids=[DstId(rid=topo.addr(c)[0], pnc=topo.addr(c)[1]) for c, _ in dests],
+            dma_engine_mask=_pick(full & ~avoid, eng),
+            remote_sem=T.sem[sem],
+            srcs=[T.xg[:, _cols(src, tiles)]],
+            dsts=[T.xg[:, _cols(slot, tiles)] for _, slot in dests],
+            alu_op=0)],
+        local_sem=T.sem.sent)
+    return eng
+
+
 def rank_program(g, core, T, topo):
-    lay, jobs, to_help, to_near, near = _plan(T, topo)
+    lay, way, jobs, calls, count = _plan(T, topo)
     rank = T.rank_of(core)
     S = T.sem
     sent = 0
@@ -91,31 +122,13 @@ def rank_program(g, core, T, topo):
         g.sync.dma_start(T.wb[:, :], T.w[:, :]).then_inc(S.ldw, 16)
 
         g.wait_ge(S.ldx, 16)
-        for dests, eng in ((to_help[core], N_HELP), (to_near[core], N_NEAR)):
-            if not dests:
-                continue
-            full = topo.mask(core, dests[0][0])
-            for c, _ in dests:
-                full &= topo.mask(core, c)
-            g.remote_dma_fused(
-                [RemoteDMATransfer(
-                    dst_ids=[DstId(rid=topo.addr(c)[0], pnc=topo.addr(c)[1]) for c, _ in dests],
-                    dma_engine_mask=_pick(full, eng),
-                    remote_sem=S.near,
-                    srcs=[T.xg[:, _cols(own)]],
-                    dsts=[T.xg[:, _cols(slot)] for _, slot in dests],
-                    alu_op=0)],
-                local_sem=S.sent)
-            sent += eng
+        for dests, eng, sem, avoid in calls[core]:
+            sent += _send(g, core, topo, T, own, dests, 1, eng, sem, avoid)
 
     if core in jobs:
-        dst, at, slot, tiles = jobs[core]
-        g.wait_ge(S.near, near[core])
-        rid, pid, _ = topo.addr(dst)
-        g.remote_dma(out_ap=T.xg[:, _cols(slot, tiles)], in_ap=T.xg[:, _cols(at, tiles)],
-                     remote_sem=S.far, local_sem=S.sent, pid=pid, routing_id=rid,
-                     dma_engine_mask=_pick(topo.mask(core, dst), N_FAR))
-        sent += N_FAR
+        g.wait_ge(S.near, count[core, "near"])
+        for (at, tiles), dests in sorted(jobs[core].items(), key=lambda e: -e[0][1]):
+            sent += _send(g, core, topo, T, at, dests, tiles, N_FAR, "far")
 
     if sent:
         g.wait_ge(S.sent, sent)
@@ -124,18 +137,16 @@ def rank_program(g, core, T, topo):
         return
 
     need = T.tables["MASK"][rank]
-    mine = topo.chip(core)
-    here = [j for j in lay[rank] if j != rank and topo.chip(T.cores[j]) == mine]
-    there = [j for j in lay[rank] if topo.chip(T.cores[j]) != mine]
     te = g.tensor
     te.wait_ge(S.ldw, 16)
     te.wait_ge(S.ldx, 16)
-    seq = [(rank, None)] + [(j, "near") for j in here] + [(j, "far") for j in there]
+    seq = [rank] + [j for kind in ("near", "dir", "far") for j in lay[rank] if j != rank and way(j, rank) == kind]
     waited = set()
-    for k, (j, sem) in enumerate(seq):
-        if sem is not None and sem not in waited:
+    for k, j in enumerate(seq):
+        sem = way(j, rank)
+        if j != rank and sem not in waited:
             waited.add(sem)
-            te.wait_ge(S[sem], near[core] if sem == "near" else N_FAR)
+            te.wait_ge(S[sem], count[core, sem])
         mm = te.matmul(T.acc[:, :], T.wb[:, _cols(need.index(j))], T.xg[:, _cols(lay[rank].index(j))],
                        k == 0, k == len(seq) - 1)
     mm.then_inc(S.mm, 1)

@@ -1,29 +1,29 @@
 from concourse.bass import DstId, RemoteDMATransfer
 
 TK = 128
+HALF = TK // 2
 DEG = 5
+SLOTS = DEG
+CAP = 2
 
-N_HELP = 8
-N_DIR = 8
-N_NEAR = 8
-N_FAR = 8
+N_ENG = 8
+N_LONG = 4
 
 SCRATCH = {
-    "xg": ("sbuf", [128, DEG * TK], "bfloat16"),
+    "xs": ("dram", [128, TK], "bfloat16"),
+    "xg": ("sbuf", [128, SLOTS * TK], "bfloat16"),
     "wb": ("sbuf", [128, DEG * TK], "bfloat16"),
-    "acc": ("psum", [128, TK], "float32"),
+    "acc0": ("psum", [128, 512], "float32"),
+    "acc1": ("psum", [128, 512], "float32"),
     "yo": ("sbuf", [128, TK], "bfloat16"),
 }
-SEMAPHORES = ["ldx", "ldw", "near", "dir", "far", "sent", "mm", "cp", "st"]
+SEMAPHORES = ["ldx", "ldo", "ldw", "hin", "near", "dir", "far0", "far1", "sent", "mm0", "mm1", "cp", "st"]
 
 
-def _pick(full, n):
-    bits = [b for b in range(full.bit_length()) if (full >> b) & 1][:n]
-    assert len(bits) == n
-    m = 0
-    for b in bits:
-        m |= 1 << b
-    return m
+def _bits(full, n):
+    bits = [b for b in range(full.bit_length()) if (full >> b) & 1]
+    assert len(bits) >= n
+    return bits[::len(bits) // n][:n]
 
 
 def _plan(T, topo):
@@ -31,104 +31,169 @@ def _plan(T, topo):
     need = T.tables["MASK"]
     n = len(cores)
     chip = [topo.chip(c) for c in cores]
+    everyone = range(topo.CHIPS * topo.CORES_PER_CHIP)
+
     def way(j, r):
         if chip[j] == chip[r]:
             return "near"
         return "dir" if topo.may_write(cores[j], cores[r]) else "far"
+
+    carrier = {}
+    helper = {}
+    for s in sorted(set(chip)):
+        def best(r):
+            return min([(topo.die(cores[q]) != topo.die(cores[r]), q) for q in range(n)
+                        if chip[q] == s and topo.may_write(cores[q], cores[r])] or [(True, None)])
+        load = {}
+        todo = [r for r in range(n) if any(way(j, r) == "far" and chip[j] == s for j in need[r])]
+        for r in sorted(todo, key=lambda r: (best(r)[0], r)):
+            tiles = [j for j in need[r] if way(j, r) == "far" and chip[j] == s]
+            q = best(r)[1]
+            if q is not None and load.get(q, 0) < CAP:
+                load[q] = load.get(q, 0) + 1
+                for j in tiles:
+                    carrier[j, r] = q
+            else:
+                for j in tiles:
+                    helper[j, r] = min((topo.die(c) != topo.die(cores[r]), c) for c in everyone
+                                       if topo.chip(c) == s and T.rank_of(c) is None and c not in helper.values()
+                                       and topo.may_write(c, cores[r]))[1]
+    carried = [sorted(set(j for (j, _), q in carrier.items() if q == p)) for p in range(n)]
+
     lay = []
     for r in range(n):
         assert r in need[r]
-        lay.append(sorted((j for j in need[r] if way(j, r) == "far"), key=lambda j: (chip[j], j))
+        lay.append(sorted((j for j in need[r] if way(j, r) == "far"), key=lambda j: (carrier.get((j, r), -1), j))
                    + sorted(j for j in need[r] if way(j, r) == "dir") + [r]
-                   + sorted(j for j in need[r] if way(j, r) == "near" and j != r))
+                   + sorted(j for j in need[r] if way(j, r) == "near" and j != r and j not in carried[r])
+                   + carried[r])
+        assert len(lay[r]) <= SLOTS
+
     jobs = {}
-    helper_in = {}
-    everyone = range(topo.CHIPS * topo.CORES_PER_CHIP)
     for r in range(n):
-        for s in sorted(set(chip[j] for j in lay[r] if way(j, r) == "far")):
-            members = [j for j in lay[r] if way(j, r) == "far" and chip[j] == s]
-            cands = []
-            for c in everyone:
-                if topo.chip(c) != s or not topo.may_write(c, cores[r]):
-                    continue
-                q = T.rank_of(c)
-                if q is None and c in jobs:
-                    continue
-                if q is not None and not all(j in lay[q] for j in members):
-                    continue
-                cands.append((topo.die(c) != topo.die(cores[r]), q is None, c))
-            _, is_helper, c = min(cands)
-            at = 0
-            if is_helper:
-                helper_in[c] = members
+        runs = []
+        for j in lay[r]:
+            if (j, r) not in carrier:
+                continue
+            q = carrier[j, r]
+            if runs and runs[-1][0] == q and lay[q].index(j) == lay[q].index(runs[-1][1][-1]) + 1:
+                runs[-1][1].append(j)
             else:
-                q = T.rank_of(c)
-                at = lay[q].index(members[0])
-                assert lay[q][at:at + len(members)] == members
-            jobs.setdefault(c, {}).setdefault((at, len(members)), []).append((cores[r], lay[r].index(members[0])))
-    calls = {}
+                runs.append((q, [j]))
+        for q, m in runs:
+            jobs.setdefault(cores[q], {}).setdefault((lay[q].index(m[0]), len(m), lay[r].index(m[0])), []).append(cores[r])
+    hop2 = {}
+    for c, job in jobs.items():
+        parts = [(at, t, to, dests) for (at, t, to), dests in sorted(job.items(), key=lambda e: -e[0][1])]
+        if len(set(p[1] for p in parts)) > 1:
+            parts = [(at + i, 1, to + i, dests) for at, t, to, dests in parts for i in range(t)]
+        writes = sum(len(p[3]) for p in parts)
+        share = [N_ENG * len(p[3]) // writes for p in parts]
+        if not (sum(share) == N_ENG and all(e > 0 and 128 % e == 0 for e in share)):
+            share = None
+        trs = [(at, t, [(d, to) for d in dests], share[i] if share else N_ENG, "far%d" % to, 0)
+               for i, (at, t, to, dests) in enumerate(parts)]
+        hop2[c] = [trs] if share else [[tr] for tr in trs]
+    for (j, r), c in helper.items():
+        to = lay[r].index(j)
+        hop2[c] = [[("xs", 1, [(cores[r], to)], N_ENG, "far%d" % to, 0)]]
+
+    hop1 = {}
+    fwd = {}
     for j in range(n):
         me = cores[j]
-        h = [(c, m.index(j)) for c, m in helper_in.items() if j in m]
-        h.sort(key=lambda e: (topo.die(e[0]) != topo.die(me), e[0]))
-        d = [(cores[r], lay[r].index(j)) for r in range(n) if j in need[r] and way(j, r) == "dir"]
-        k = [(cores[r], lay[r].index(j)) for r in range(n) if j in need[r] and r != j and way(j, r) == "near"]
-        k.sort(key=lambda e: (e[0] not in jobs, e[0]))
+        h = sorted((c, "xs") for (i, _), c in helper.items() if i == j)
+        a = [(cores[q], lay[q].index(j)) for q in range(n) if q != j and j in carried[q]]
+        d = [r for r in range(n) if j in need[r] and way(j, r) == "dir"]
+        free = sorted((topo.die(cores[r]) != topo.die(me), r) for r in d if cores[r] not in hop2)
+        if free and len(d) > 1:
+            f = free[0][1]
+            fwd.setdefault(cores[f], []).append(
+                [(lay[f].index(j), 1, [(cores[r], lay[r].index(j)) for r in d if r != f], N_ENG, "dir", 0)])
+            d = [f]
+        d = [(cores[r], lay[r].index(j)) for r in d]
+        k = [(cores[r], lay[r].index(j)) for r in range(n)
+             if j in need[r] and r != j and way(j, r) == "near" and j not in carried[r]]
         off = 0
+        for call in hop2.get(me, []):
+            for tr in call:
+                for c, _ in tr[2]:
+                    off |= topo.mask(me, c)
         for c, _ in d:
             off |= topo.mask(me, c)
-        calls[me] = [c for c in ((h, N_HELP, "near", off), (d, N_DIR, "dir", 0), (k, N_NEAR, "near", off)) if c[0]]
+        hop1[me] = [[("xs", 1, dests, e, sem, avoid)] for dests, e, sem, avoid in
+                    ((h, N_LONG, "hin", off), (a, N_ENG, "near", off), (d, N_ENG, "dir", 0), (k, N_ENG, "near", off))
+                    if dests]
+
     count = {}
-    for me in cores:
-        for dests, eng, sem, _ in calls[me]:
-            for c, _ in dests:
-                count[c, sem] = count.get((c, sem), 0) + eng
-    for c in jobs:
-        for dests in jobs[c].values():
-            for d, _ in dests:
-                count[d, "far"] = count.get((d, "far"), 0) + N_FAR
-    return lay, way, jobs, calls, count
+    for plan in (hop1, fwd, hop2):
+        for calls in plan.values():
+            for call in calls:
+                for _, _, dests, e, sem, _ in call:
+                    for c, _ in dests:
+                        count[c, sem] = count.get((c, sem), 0) + e
+    return lay, way, hop1, fwd, hop2, count
 
 
 def _cols(first, tiles=1):
     return slice(first * TK, (first + tiles) * TK)
 
 
-def _send(g, core, topo, T, src, dests, tiles, eng, sem, avoid=0):
-    full = topo.mask(core, dests[0][0])
-    for c, _ in dests:
-        full &= topo.mask(core, c)
-    g.remote_dma_fused(
-        [RemoteDMATransfer(
+def _side(T, at, tiles):
+    return T.xs[:, :] if at == "xs" else T.xg[:, _cols(at, tiles)]
+
+
+def _send(g, core, topo, T, call):
+    full = ~0
+    for _, _, dests, _, _, avoid in call:
+        for c, _ in dests:
+            full &= topo.mask(core, c)
+        full &= ~avoid
+    total = sum(tr[3] for tr in call)
+    bits = _bits(full, total)
+    trs = []
+    for src, tiles, dests, e, sem, _ in call:
+        m = 0
+        for b in bits[:e]:
+            m |= 1 << b
+        bits = bits[e:]
+        trs.append(RemoteDMATransfer(
             dst_ids=[DstId(rid=topo.addr(c)[0], pnc=topo.addr(c)[1]) for c, _ in dests],
-            dma_engine_mask=_pick(full & ~avoid, eng),
+            dma_engine_mask=m,
             remote_sem=T.sem[sem],
-            srcs=[T.xg[:, _cols(src, tiles)]],
-            dsts=[T.xg[:, _cols(slot, tiles)] for _, slot in dests],
-            alu_op=0)],
-        local_sem=T.sem.sent)
-    return eng
+            srcs=[_side(T, src, tiles)],
+            dsts=[_side(T, to, tiles) for _, to in dests],
+            alu_op=0))
+    g.remote_dma_fused(trs, local_sem=T.sem.sent)
+    return total
 
 
 def rank_program(g, core, T, topo):
-    lay, way, jobs, calls, count = _plan(T, topo)
+    lay, way, hop1, fwd, hop2, count = _plan(T, topo)
     rank = T.rank_of(core)
     S = T.sem
     sent = 0
 
     if rank is not None:
         own = lay[rank].index(rank)
-        g.sync.dma_start(T.xg[:, _cols(own)], T.x[:, :]).then_inc(S.ldx, 16)
+        g.sync.dma_start(T.xs[:, :], T.x[:, :]).then_inc(S.ldx, 16)
+        g.sync.dma_start(T.xg[:, _cols(own)], T.x[:, :]).then_inc(S.ldo, 16)
         g.sync.dma_start(T.wb[:, :], T.w[:, :]).then_inc(S.ldw, 16)
 
         g.wait_ge(S.ldx, 16)
-        for dests, eng, sem, avoid in calls[core]:
-            sent += _send(g, core, topo, T, own, dests, 1, eng, sem, avoid)
+        for call in hop1[core]:
+            sent += _send(g, core, topo, T, call)
 
-    if core in jobs:
-        g.wait_ge(S.near, count[core, "near"])
-        for (at, tiles), dests in sorted(jobs[core].items(), key=lambda e: -e[0][1]):
-            sent += _send(g, core, topo, T, at, dests, tiles, N_FAR, "far")
+    if core in fwd:
+        g.wait_ge(S.dir, count[core, "dir"])
+        for call in fwd[core]:
+            sent += _send(g, core, topo, T, call)
+
+    if core in hop2:
+        sem = "hin" if rank is None else "near"
+        g.wait_ge(S[sem], count[core, sem])
+        for call in hop2[core]:
+            sent += _send(g, core, topo, T, call)
 
     if sent:
         g.wait_ge(S.sent, sent)
@@ -137,23 +202,32 @@ def rank_program(g, core, T, topo):
         return
 
     need = T.tables["MASK"][rank]
+    acc = (T.acc0, T.acc1)
     te = g.tensor
     te.wait_ge(S.ldw, 16)
-    te.wait_ge(S.ldx, 16)
-    seq = [rank] + [j for kind in ("near", "dir", "far") for j in lay[rank] if j != rank and way(j, rank) == kind]
+    te.wait_ge(S.ldo, 16)
+    seq = [rank] + [j for kind in ("near", "dir", "far") for j in lay[rank]
+                    if j != rank and j in need and way(j, rank) == kind]
     waited = set()
     for k, j in enumerate(seq):
+        slot = lay[rank].index(j)
         sem = way(j, rank)
-        if j != rank and sem not in waited:
+        if sem == "far":
+            sem = "far%d" % slot
+        if j != rank and sem not in waited and (core, sem) in count:
             waited.add(sem)
             te.wait_ge(S[sem], count[core, sem])
-        mm = te.matmul(T.acc[:, :], T.wb[:, _cols(need.index(j))], T.xg[:, _cols(lay[rank].index(j))],
-                       k == 0, k == len(seq) - 1)
-    mm.then_inc(S.mm, 1)
+        last = k == len(seq) - 1
+        for h in range(2):
+            mm = te.matmul(acc[h][:, 0:HALF], T.wb[:, _cols(need.index(j))],
+                           T.xg[:, slot * TK + h * HALF:slot * TK + (h + 1) * HALF], k == 0, last)
+            if last:
+                mm.then_inc(S["mm%d" % h], 1)
 
-    g.vector.wait_ge(S.mm, 1)
-    g.vector.tensor_copy(T.yo[:, :], T.acc[:, :]).then_inc(S.cp, 1)
+    for h in range(2):
+        g.vector.wait_ge(S["mm%d" % h], 1)
+        g.vector.tensor_copy(T.yo[:, h * HALF:(h + 1) * HALF], acc[h][:, 0:HALF]).then_inc(S.cp, 1)
 
-    g.scalar.wait_ge(S.cp, 1)
+    g.scalar.wait_ge(S.cp, 2)
     g.scalar.dma_start(T.y[:, :], T.yo[:, :]).then_inc(S.st, 16)
     g.scalar.wait_ge(S.st, 16)

from concourse.bass import DstId, RemoteDMATransfer

TK = 128
HALF = TK // 2
DEG = 5
SLOTS = DEG
CAP = 2

N_ENG = 8
N_LONG = 4

SCRATCH = {
    "xs": ("dram", [128, TK], "bfloat16"),
    "xg": ("sbuf", [128, SLOTS * TK], "bfloat16"),
    "wb": ("sbuf", [128, DEG * TK], "bfloat16"),
    "acc0": ("psum", [128, 512], "float32"),
    "acc1": ("psum", [128, 512], "float32"),
    "yo": ("sbuf", [128, TK], "bfloat16"),
}
SEMAPHORES = ["ldx", "ldo", "ldw", "hin", "near", "dir", "far0", "far1", "sent", "mm0", "mm1", "cp", "st"]


def _bits(full, n):
    bits = [b for b in range(full.bit_length()) if (full >> b) & 1]
    assert len(bits) >= n
    return bits[::len(bits) // n][:n]


def _plan(T, topo):
    cores = list(T.cores)
    need = T.tables["MASK"]
    n = len(cores)
    chip = [topo.chip(c) for c in cores]
    everyone = range(topo.CHIPS * topo.CORES_PER_CHIP)

    def way(j, r):
        if chip[j] == chip[r]:
            return "near"
        return "dir" if topo.may_write(cores[j], cores[r]) else "far"

    carrier = {}
    helper = {}
    for s in sorted(set(chip)):
        def best(r):
            return min([(topo.die(cores[q]) != topo.die(cores[r]), q) for q in range(n)
                        if chip[q] == s and topo.may_write(cores[q], cores[r])] or [(True, None)])
        load = {}
        todo = [r for r in range(n) if any(way(j, r) == "far" and chip[j] == s for j in need[r])]
        for r in sorted(todo, key=lambda r: (best(r)[0], r)):
            tiles = [j for j in need[r] if way(j, r) == "far" and chip[j] == s]
            q = best(r)[1]
            if q is not None and load.get(q, 0) < CAP:
                load[q] = load.get(q, 0) + 1
                for j in tiles:
                    carrier[j, r] = q
            else:
                for j in tiles:
                    helper[j, r] = min((topo.die(c) != topo.die(cores[r]), c) for c in everyone
                                       if topo.chip(c) == s and T.rank_of(c) is None and c not in helper.values()
                                       and topo.may_write(c, cores[r]))[1]
    carried = [sorted(set(j for (j, _), q in carrier.items() if q == p)) for p in range(n)]

    lay = []
    for r in range(n):
        assert r in need[r]
        lay.append(sorted((j for j in need[r] if way(j, r) == "far"), key=lambda j: (carrier.get((j, r), -1), j))
                   + sorted(j for j in need[r] if way(j, r) == "dir") + [r]
                   + sorted(j for j in need[r] if way(j, r) == "near" and j != r and j not in carried[r])
                   + carried[r])
        assert len(lay[r]) <= SLOTS

    jobs = {}
    for r in range(n):
        runs = []
        for j in lay[r]:
            if (j, r) not in carrier:
                continue
            q = carrier[j, r]
            if runs and runs[-1][0] == q and lay[q].index(j) == lay[q].index(runs[-1][1][-1]) + 1:
                runs[-1][1].append(j)
            else:
                runs.append((q, [j]))
        for q, m in runs:
            jobs.setdefault(cores[q], {}).setdefault((lay[q].index(m[0]), len(m), lay[r].index(m[0])), []).append(cores[r])
    hop2 = {}
    for c, job in jobs.items():
        parts = [(at, t, to, dests) for (at, t, to), dests in sorted(job.items(), key=lambda e: -e[0][1])]
        if len(set(p[1] for p in parts)) > 1:
            parts = [(at + i, 1, to + i, dests) for at, t, to, dests in parts for i in range(t)]
        writes = sum(len(p[3]) for p in parts)
        share = [N_ENG * len(p[3]) // writes for p in parts]
        if not (sum(share) == N_ENG and all(e > 0 and 128 % e == 0 for e in share)):
            share = None
        trs = [(at, t, [(d, to) for d in dests], share[i] if share else N_ENG, "far%d" % to, 0)
               for i, (at, t, to, dests) in enumerate(parts)]
        hop2[c] = [trs] if share else [[tr] for tr in trs]
    for (j, r), c in helper.items():
        to = lay[r].index(j)
        hop2[c] = [[("xs", 1, [(cores[r], to)], N_ENG, "far%d" % to, 0)]]

    hop1 = {}
    fwd = {}
    for j in range(n):
        me = cores[j]
        h = sorted((c, "xs") for (i, _), c in helper.items() if i == j)
        a = [(cores[q], lay[q].index(j)) for q in range(n) if q != j and j in carried[q]]
        d = [r for r in range(n) if j in need[r] and way(j, r) == "dir"]
        free = sorted((topo.die(cores[r]) != topo.die(me), r) for r in d if cores[r] not in hop2)
        if free and len(d) > 1:
            f = free[0][1]
            fwd.setdefault(cores[f], []).append(
                [(lay[f].index(j), 1, [(cores[r], lay[r].index(j)) for r in d if r != f], N_ENG, "dir", 0)])
            d = [f]
        d = [(cores[r], lay[r].index(j)) for r in d]
        k = [(cores[r], lay[r].index(j)) for r in range(n)
             if j in need[r] and r != j and way(j, r) == "near" and j not in carried[r]]
        off = 0
        for call in hop2.get(me, []):
            for tr in call:
                for c, _ in tr[2]:
                    off |= topo.mask(me, c)
        for c, _ in d:
            off |= topo.mask(me, c)
        hop1[me] = [[("xs", 1, dests, e, sem, avoid)] for dests, e, sem, avoid in
                    ((h, N_LONG, "hin", off), (a, N_ENG, "near", off), (d, N_ENG, "dir", 0), (k, N_ENG, "near", off))
                    if dests]

    count = {}
    for plan in (hop1, fwd, hop2):
        for calls in plan.values():
            for call in calls:
                for _, _, dests, e, sem, _ in call:
                    for c, _ in dests:
                        count[c, sem] = count.get((c, sem), 0) + e
    return lay, way, hop1, fwd, hop2, count


def _cols(first, tiles=1):
    return slice(first * TK, (first + tiles) * TK)


def _side(T, at, tiles):
    return T.xs[:, :] if at == "xs" else T.xg[:, _cols(at, tiles)]


def _send(g, core, topo, T, call):
    full = ~0
    for _, _, dests, _, _, avoid in call:
        for c, _ in dests:
            full &= topo.mask(core, c)
        full &= ~avoid
    total = sum(tr[3] for tr in call)
    bits = _bits(full, total)
    trs = []
    for src, tiles, dests, e, sem, _ in call:
        m = 0
        for b in bits[:e]:
            m |= 1 << b
        bits = bits[e:]
        trs.append(RemoteDMATransfer(
            dst_ids=[DstId(rid=topo.addr(c)[0], pnc=topo.addr(c)[1]) for c, _ in dests],
            dma_engine_mask=m,
            remote_sem=T.sem[sem],
            srcs=[_side(T, src, tiles)],
            dsts=[_side(T, to, tiles) for _, to in dests],
            alu_op=0))
    g.remote_dma_fused(trs, local_sem=T.sem.sent)
    return total


def rank_program(g, core, T, topo):
    lay, way, hop1, fwd, hop2, count = _plan(T, topo)
    rank = T.rank_of(core)
    S = T.sem
    sent = 0

    if rank is not None:
        own = lay[rank].index(rank)
        g.sync.dma_start(T.xs[:, :], T.x[:, :]).then_inc(S.ldx, 16)
        g.sync.dma_start(T.xg[:, _cols(own)], T.x[:, :]).then_inc(S.ldo, 16)
        g.sync.dma_start(T.wb[:, :], T.w[:, :]).then_inc(S.ldw, 16)

        g.wait_ge(S.ldx, 16)
        for call in hop1[core]:
            sent += _send(g, core, topo, T, call)

    if core in fwd:
        g.wait_ge(S.dir, count[core, "dir"])
        for call in fwd[core]:
            sent += _send(g, core, topo, T, call)

    if core in hop2:
        sem = "hin" if rank is None else "near"
        g.wait_ge(S[sem], count[core, sem])
        for call in hop2[core]:
            sent += _send(g, core, topo, T, call)

    if sent:
        g.wait_ge(S.sent, sent)

    if rank is None:
        return

    need = T.tables["MASK"][rank]
    acc = (T.acc0, T.acc1)
    te = g.tensor
    te.wait_ge(S.ldw, 16)
    te.wait_ge(S.ldo, 16)
    seq = [rank] + [j for kind in ("near", "dir", "far") for j in lay[rank]
                    if j != rank and j in need and way(j, rank) == kind]
    waited = set()
    for k, j in enumerate(seq):
        slot = lay[rank].index(j)
        sem = way(j, rank)
        if sem == "far":
            sem = "far%d" % slot
        if j != rank and sem not in waited and (core, sem) in count:
            waited.add(sem)
            te.wait_ge(S[sem], count[core, sem])
        last = k == len(seq) - 1
        for h in range(2):
            mm = te.matmul(acc[h][:, 0:HALF], T.wb[:, _cols(need.index(j))],
                           T.xg[:, slot * TK + h * HALF:slot * TK + (h + 1) * HALF], k == 0, last)
            if last:
                mm.then_inc(S["mm%d" % h], 1)

    for h in range(2):
        g.vector.wait_ge(S["mm%d" % h], 1)
        g.vector.tensor_copy(T.yo[:, h * HALF:(h + 1) * HALF], acc[h][:, 0:HALF]).then_inc(S.cp, 1)

    g.scalar.wait_ge(S.cp, 2)
    g.scalar.dma_start(T.y[:, :], T.yo[:, :]).then_inc(S.st, 16)
    g.scalar.wait_ge(S.st, 16)
